import numpy as np
import ml_dtypes


def mxq(x, axis, fmt="e4m3"):
    dtype, down = {"e4m3": (ml_dtypes.float8_e4m3fn, 7), "e5m2": (ml_dtypes.float8_e5m2, 14)}[fmt]
    v = np.moveaxis(np.asarray(x, np.float32).astype(ml_dtypes.bfloat16).astype(np.float64), axis, -1)
    blocks = v.reshape(v.shape[:-1] + (-1, 32))
    amax = np.abs(blocks).max(-1, keepdims=True)
    byte = np.maximum(np.where(amax > 0, np.frexp(amax)[1] - 1 + 127, 0) - down, 1)
    scale = np.exp2(byte - 127.0)
    codes = (blocks / scale).astype(np.float32).astype(dtype).astype(np.float64)
    return np.moveaxis((codes * scale).reshape(v.shape), -1, axis)


WIDE = False


def mx_kscale(k):
    if not WIDE:
        return np.ones(k)
    levels = np.array([10, -10, 5, -5, 0])
    if k % 512:
        return np.exp2(np.random.permutation(np.resize(levels, k // 32))).repeat(32)
    a = np.empty((k // 512, 16))
    for p in range(k // 512):
        a[p, :8] = np.random.permutation(np.resize(levels, 8))
        for g in range(8):
            far = levels[np.abs(levels - a[p, g]) >= 10]
            a[p, g + 8] = far[np.random.randint(len(far))]
    return np.exp2(a.ravel()).repeat(32)


BF16 = ml_dtypes.bfloat16


def bf(x):
    return np.asarray(x, np.float32).astype(BF16)


def f64(x):
    return np.asarray(x).astype(np.float64)


E2M1 = np.array([0.0, 0.5, 1.0, 1.5, 2.0, 3.0, 4.0, 6.0, -0.0, -0.5, -1.0, -1.5, -2.0, -3.0, -4.0, -6.0])


def pack_weight(w, fmt):
    k, n = w.shape
    w = f64(bf(w)).reshape(k // 32, 32, n)
    amax = np.abs(w).max(1)
    if fmt == "e4m3":
        byte = np.frexp(amax)[1] - 1 + 127 - 7
    else:
        mant, ex = np.frexp(amax / 6.0)
        byte = np.where(mant > 0.5, ex, ex - 1) + 127
    byte = np.clip(np.where(amax > 0, byte, 1), 1, 254)
    scaled = (w * np.exp2(127.0 - byte)[:, None, :]).reshape(k, n).astype(np.float32)
    by_word = np.ascontiguousarray(scaled.reshape(k // 512, 128, 4, n).transpose(0, 1, 3, 2))
    if fmt == "e4m3":
        words = by_word.astype(ml_dtypes.float8_e4m3fn).view(np.uint8)
    else:
        c = by_word.astype(ml_dtypes.float4_e2m1fn).view(np.uint8) & 0xF
        words = c[..., 0::2] | (c[..., 1::2] << 4)
    return np.ascontiguousarray(words), np.ascontiguousarray(byte.astype(np.uint8).reshape(k // 512, 16, n))


def unpack_weight(words, scales, fmt):
    g, p, n, _ = words.shape
    if fmt == "e4m3":
        vals = np.ascontiguousarray(words).view(ml_dtypes.float8_e4m3fn).astype(np.float64)
    else:
        nib = np.empty((g, p, n, 4), np.uint8)
        nib[..., 0::2] = words & 0xF
        nib[..., 1::2] = words >> 4
        vals = E2M1[nib]
    vals = vals * np.repeat(np.exp2(scales.astype(np.float64) - 127.0), 8, axis=1)[..., None]
    return vals.transpose(0, 1, 3, 2).reshape(g * 512, n)
def pack4(w):
    words, scales = pack_weight(w, "e2m1")
    return words.reshape(words.shape[0], 128, -1), scales


def unpack4(words, scales):
    return unpack_weight(words.reshape(words.shape[0], 128, -1, 2), scales, "e2m1")


def planes(Y):
    n, m = Y.shape
    b = f64(bf(Y)).reshape(n // 32, 32, m)
    amax = np.abs(b).max(1)
    byte = np.clip(np.where(amax > 0, np.frexp(amax)[1] - 1 + 127 - 7, 1), 1, 254)
    codes = (b * np.exp2(127.0 - byte)[:, None, :]).reshape(n, m).astype(np.float32).astype(ml_dtypes.float8_e4m3fn).view(np.uint8)
    words = codes.reshape(n // 512, 128, 4, m).transpose(0, 1, 3, 2)
    return np.ascontiguousarray(words), np.ascontiguousarray(byte.astype(np.uint8).reshape(n // 512, 16, m))


M, K, N = 768, 1024, 1536
KAPPA = 0.3 * np.sqrt(K)

def unit_columns(z):
    return z / np.sqrt((z * z).sum(axis=0, keepdims=True))

def setup_inputs():
    s = mx_kscale(K)[:, None]
    x = unit_columns(np.random.randn(K, M))
    base = np.random.randn(K, N)
    a = KAPPA * unit_columns(base + np.random.randn(K, N))
    b = KAPPA * unit_columns(base + np.random.randn(K, N))
    c = KAPPA * unit_columns(base + np.random.randn(K, N))
    w = np.exp(0.8 * np.random.randn(N))
    gain = w / (w.mean() * np.exp(0.5 * 6.0 * KAPPA ** 2 / K))
    x_words, x_scales = pack_weight(x * s, "e4m3")
    a_words, a_scales = pack4(a / s)
    b_words, b_scales = pack_weight(b / s, "e4m3")
    return {"x_words": x_words, "x_scales": x_scales,
            "a_words": a_words, "a_scales": a_scales,
            "b_words": b_words, "b_scales": b_scales,
            "c": bf(c / s), "gain": bf(gain)}

def reference(x_words, x_scales, a_words, a_scales, b_words, b_scales, c, gain):
    xt = unpack_weight(x_words, x_scales, "e4m3").T
    wa = unpack4(a_words, a_scales)
    wb = unpack_weight(b_words, b_scales, "e4m3")
    wc = mxq(f64(c), 0, "e4m3")
    sa = xt @ wa
    sb = xt @ wb
    sc = xt @ wc
    y = np.exp(sa + sb + sc) * f64(gain)
    words, scales = planes(y.T)
    return y, words, scales

@@ -1,0 +1,318 @@
+from contextlib import ExitStack
+
+import concourse.mybir as mybir
+from concourse.masks import make_identity
+
+M, K, N = 768, 1024, 1536
+FLOPS = 3 * 2 * M * K * N
+
+F32 = mybir.dt.float32
+BF16 = mybir.dt.bfloat16
+I32 = mybir.dt.int32
+U32 = mybir.dt.uint32
+U8 = mybir.dt.uint8
+FP8X4 = mybir.dt.float8_e4m3fn_x4
+FP4X4 = mybir.dt.float4_e2m1fn_x4
+ACT = mybir.ActivationFunctionType
+ALU = mybir.AluOpType
+
+P = 128
+PACK = 4
+GROUPS = K // (P * PACK)
+WIDE = 512
+CHUNKS = N // WIDE
+ROWS = M // P
+TILES = CHUNKS * ROWS
+C_SPLIT = 256
+
+
+def tile_uniformity_pair_weights_k3_kernel(
+    tc, x_words, x_scales, a_words, a_scales, b_words, b_scales, c, gain, out_0, out_1, out_2
+):
+    nc = tc.nc
+    with ExitStack() as ctx:
+        keep = ctx.enter_context(tc.tile_pool(name="keep", bufs=1))
+        psum = ctx.enter_context(tc.psum_pool(name="psum", bufs=1))
+        ctx.enter_context(tc.manual_schedule())
+
+        def sb(name, shape, dtype):
+            t = keep.tile(shape, dtype, name=name, tag=name, align_bytes=64)
+            return t
+
+        def bank(i, shape):
+            t = psum.tile(shape, F32, name="bank%d" % i, tag="bank%d" % i)
+            return t
+
+        x_sc = sb("x_sc", [P, GROUPS, M], U8)
+        a_sc = sb("a_sc", [P, GROUPS, N], U8)
+        b_sc = sb("b_sc", [P, GROUPS, N], U8)
+        x_w = [sb("x_w%d" % g, [P, M], U32) for g in range(GROUPS)]
+        a_w = [sb("a_w%d" % j, [P, GROUPS, 2 * WIDE], U8) for j in range(CHUNKS)]
+        b_w = [sb("b_w%d" % j, [P, GROUPS, WIDE], U32) for j in range(CHUNKS)]
+        pieces = [(j, g) for j in range(CHUNKS) for g in range(GROUPS)]
+        c_raw = {k: sb("c_raw%d%d" % k, [P, PACK, WIDE], BF16) for k in pieces}
+        c_grp = {k: sb("c_grp%d%d" % k, [P, WIDE, PACK], BF16) for k in pieces}
+        c_w = {k: sb("c_w%d%d" % k, [P, WIDE], U32) for k in pieces}
+        c_sc = {k: sb("c_sc%d%d" % k, [P, WIDE], U8) for k in pieces}
+        zeros = sb("zeros", [P, P], BF16)
+        ones = sb("ones", [P, P], BF16)
+        gain_row = sb("gain_row", [P, N], BF16)
+        gain_all = sb("gain_all", [P, N], F32)
+        ident = sb("ident", [P, P], F32)
+        e_t = [sb("e%d" % i, [P, WIDE], F32) for i in range(TILES)]
+        y_t = [sb("y%d" % i, [P, WIDE], F32) for i in range(TILES)]
+        y_bf = [sb("ybf%d" % i, [P, WIDE], BF16) for i in range(TILES)]
+        y_grp = [sb("ygrp%d" % j, [P, M * PACK], BF16) for j in range(CHUNKS)]
+        y_w = [sb("y_w%d" % j, [P, M], U32) for j in range(CHUNKS)]
+        y_sc = sb("y_sc", [P, CHUNKS, M], U8)
+
+        def zero(t):
+            nc.vector.memset(t.bitcast(I32), 0)
+
+        def load_scales(plane, rows, r):
+            src = rows.rearrange("g (q r) n -> r q g n", r=4)[r]
+            nc.sync.dma_start(out=plane[r:P:32, :, :].bitcast(I32), in_=src.bitcast(I32))
+
+        def load_x(eng, g):
+            eng.dma_start(out=x_w[g][:].bitcast(I32), in_=x_words[g].rearrange("p m t -> p (m t)").bitcast(I32))
+
+        def load_a(eng, j):
+            src = a_words.rearrange("g p n -> p g n")[:, :, 2 * WIDE * j : 2 * WIDE * (j + 1)]
+            eng.dma_start(out=a_w[j][:].bitcast(I32), in_=src.bitcast(I32))
+
+        def load_b(j):
+            src = b_words.rearrange("g p n t -> p g (n t)")[:, :, PACK * WIDE * j : PACK * WIDE * (j + 1)]
+            nc.sync.dma_start(out=b_w[j][:].bitcast(I32), in_=src.bitcast(I32))
+
+        def load_c(j, g):
+            src = c[P * PACK * g : P * PACK * (g + 1), WIDE * j : WIDE * (j + 1)]
+            nc.sync.dma_start(out=c_raw[j, g][:], in_=src.rearrange("(p t) n -> p t n", t=PACK))
+
+        def weave(j, g, lo, hi):
+            dst = c_grp[j, g][:, lo:hi, :].rearrange("p (n i) t -> p n t i", i=4)
+            src = c_raw[j, g][:, :, lo:hi].rearrange("p t (n i) -> p n t i", i=4)
+            return dst, src
+
+        def weave_v(j, g):
+            dst, src = weave(j, g, 0, C_SPLIT)
+            nc.vector.tensor_copy(out=dst, in_=src)
+
+        def weave_s(j, g):
+            dst, src = weave(j, g, C_SPLIT, WIDE)
+            nc.scalar.copy(out=dst, in_=src)
+
+        def quant_c(j, g):
+            nc.vector.quantize_mx(
+                out=c_w[j, g][:].bitcast(FP8X4),
+                scales=c_sc[j, g][:],
+                in_=c_grp[j, g][:].rearrange("p n t -> p (n t)"),
+            )
+
+        acc = {}
+
+        def mx(i, which, g):
+            j, mt = divmod(i, ROWS)
+            ms = slice(P * mt, P * (mt + 1))
+            ns = slice(WIDE * j, WIDE * (j + 1))
+            if which == "a":
+                rhs, rhs_sc = a_w[j][:, g, :].bitcast(FP4X4), a_sc[:, g, ns]
+            elif which == "b":
+                rhs, rhs_sc = b_w[j][:, g, :].bitcast(FP8X4), b_sc[:, g, ns]
+            else:
+                rhs, rhs_sc = c_w[j, g][:].bitcast(FP8X4), c_sc[j, g][:]
+            first = which == "a" and g == 0
+            if first:
+                acc[i] = bank(i if i < 8 else MX_RING[(i - 6) % len(MX_RING)], [P, WIDE])
+            nc.tensor.matmul_mx(
+                out=acc[i][:],
+                lhsT=x_w[g][:, ms].bitcast(FP8X4),
+                lhsT_scale=x_sc[:, g, ms],
+                rhs=rhs,
+                rhs_scale=rhs_sc,
+                start=first,
+                stop=(which == "c" and g == GROUPS - 1),
+            )
+
+        def mx_tile(i):
+            for which in "abc":
+                for g in range(GROUPS):
+                    mx(i, which, g)
+
+        def exp(i):
+            nc.scalar.activation(out=e_t[i][:], in_=acc[i][:], func=ACT.Exp)
+
+        def mul(i):
+            j, mt = divmod(i, ROWS)
+            nc.vector.tensor_tensor(
+                out=y_t[i][:], in0=e_t[i][:], in1=gain_all[:, WIDE * j : WIDE * (j + 1)], op=ALU.mult
+            )
+            nc.sync.dma_start(out=out_0[P * mt : P * (mt + 1), WIDE * j : WIDE * (j + 1)], in_=y_t[i][:])
+
+        def cast(i):
+            nc.vector.tensor_copy(
+                out=y_bf[i][:].rearrange("m (u p e) -> m u p e", u=2, e=2),
+                in_=y_t[i][:].rearrange("m (p u e) -> m u p e", u=2, e=2),
+            )
+
+        turned = {}
+
+        def turn(i, count, b):
+            turned[i] = bank(b, [P, count, 2, P])
+            for s in range(count):
+                words = y_bf[i + s][:].bitcast(F32)
+                for u in range(2):
+                    nc.tensor.transpose(turned[i][:, s, u, :], words[:, P * u : P * (u + 1)], ident[:])
+
+        def grp_cols(i, count):
+            mt = i % ROWS
+            return y_grp[i // ROWS][:, P * PACK * mt : P * PACK * (mt + count)]
+
+        def evac(i, count):
+            nc.scalar.copy(
+                out=grp_cols(i, count).bitcast(F32).rearrange("p (s m u) -> p s m u", s=count, u=2),
+                in_=turned[i][:].rearrange("p s u m -> p s m u"),
+            )
+
+        def quant_y(i, count):
+            j, mt = divmod(i, ROWS)
+            ms = slice(P * mt, P * (mt + count))
+            nc.vector.quantize_mx(out=y_w[j][:, ms].bitcast(FP8X4), scales=y_sc[:, j, ms], in_=grp_cols(i, count))
+
+        def store_words(j, lo, hi):
+            dst = out_1[j].rearrange("p m t -> p (m t)").bitcast(I32)
+            nc.sync.dma_start(out=dst[:, lo:hi], in_=y_w[j][:, lo:hi].bitcast(I32))
+
+        def store_scales(eng, r, lo, hi):
+            dst = out_2.rearrange("g (q r) m -> r q g m", r=4)[r]
+            eng.dma_start(out=dst[:, lo:hi, :].bitcast(I32), in_=y_sc[r:P:32, lo:hi, :].bitcast(I32))
+
+        nc.vector.memset(zeros[:], 0.0)
+        zero(x_sc[:])
+        nc.vector.memset(gain_row[:], 0.0)
+        zero(a_sc[:])
+        zero(b_sc[:])
+        nc.scalar.activation(out=ones[:], in_=zeros[:], func=ACT.Exp)
+        load_x(nc.gpsimd, 0)
+        load_a(nc.gpsimd, 0)
+        make_identity(nc, ident[:])
+        for r in range(4):
+            load_scales(x_sc, x_scales, r)
+        nc.sync.dma_start(out=gain_row[0:1, :], in_=gain.rearrange("(o n) -> o n", o=1))
+        for r in range(4):
+            load_scales(a_sc, a_scales, r)
+        load_x(nc.sync, 1)
+        load_b(0)
+        for r in range(4):
+            load_scales(b_sc, b_scales, r)
+        load_c(0, 0)
+        load_c(0, 1)
+        load_c(1, 0)
+        load_c(1, 1)
+        load_a(nc.sync, 1)
+        load_b(1)
+        load_c(2, 0)
+        load_c(2, 1)
+        load_a(nc.sync, 2)
+        load_b(2)
+
+        for j in range(CHUNKS):
+            ns = slice(WIDE * j, WIDE * (j + 1))
+            spread = bank(5 + j, [P, WIDE])
+            nc.tensor.matmul(spread[:], lhsT=ones[:], rhs=gain_row[:, ns], start=True, stop=True)
+            nc.scalar.copy(out=gain_all[:, ns], in_=spread[:])
+
+        for j in range(2):
+            for g in range(GROUPS):
+                weave_s(j, g)
+                weave_v(j, g)
+                quant_c(j, g)
+
+        for which in "abc":
+            for g in range(GROUPS):
+                for i in range(ROWS):
+                    mx(i, which, g)
+        for i in range(ROWS):
+            exp(i)
+            mul(i)
+            if i > 0:
+                cast(i - 1)
+
+        mx_tile(6)
+        weave_s(2, 0)
+        weave_v(2, 0)
+        cast(5)
+        quant_c(2, 0)
+        exp(6)
+        mul(6)
+        weave_s(2, 1)
+        weave_v(2, 1)
+        cast(6)
+        quant_c(2, 1)
+        for i in range(7, 11):
+            mx_tile(i)
+            exp(i)
+            mul(i)
+            if i > 7:
+                cast(i - 1)
+        for s in range(3):
+            turn(2 * s, 2, 3 + s)
+        for s in range(3):
+            evac(2 * s, 2)
+        quant_y(0, 2)
+        cast(10)
+        quant_y(2, 2)
+        mx_tile(11)
+        exp(11)
+        mul(11)
+        quant_y(4, 2)
+        store_words(0, 0, M)
+        cast(11)
+
+        mx_tile(12)
+        exp(12)
+        mul(12)
+        mx_tile(13)
+        exp(13)
+        mul(13)
+        cast(12)
+        for s in range(3):
+            turn(6 + 2 * s, 2, 3 + s)
+        for s in range(3):
+            evac(6 + 2 * s, 2)
+        quant_y(6, 2)
+        cast(13)
+        quant_y(8, 2)
+        mx_tile(14)
+        exp(14)
+        mul(14)
+        quant_y(10, 2)
+        store_words(1, 0, M)
+        for r in range(4):
+            store_scales(nc.sync, r, 0, 2)
+        cast(14)
+        for i in range(15, 18):
+            mx_tile(i)
+            exp(i)
+            mul(i)
+            cast(i)
+        turn(12, 2, 3)
+        turn(14, 2, 4)
+        turn(16, 1, 5)
+        turn(17, 1, 2)
+        evac(12, 2)
+        evac(14, 2)
+        evac(16, 1)
+        evac(17, 1)
+        quant_y(12, 2)
+        quant_y(14, 2)
+        store_words(2, 0, 4 * P)
+        quant_y(16, 1)
+        quant_y(17, 1)
+        store_words(2, 4 * P, M)
+        store_scales(nc.scalar, 0, 2, 3)
+        store_scales(nc.sync, 1, 2, 3)
+        store_scales(nc.scalar, 2, 2, 3)
+        store_scales(nc.sync, 3, 2, 3)
+
+
+MX_RING = [6, 7, 0, 1, 2]

@@ -23,6 +23,8 @@ WIDE = 512
 CHUNKS = N // WIDE
 ROWS = M // P
 TILES = CHUNKS * ROWS
+B_ROW = 4
+MX_BANK = [0, 1, 2, 3, 4, 5, 6, 7, 0, 1, 2, 6, 7, 0, 1, 6, 7, 0]
 C_SPLIT = 256
 
 
@@ -44,8 +46,8 @@ def tile_uniformity_pair_weights_k3_kernel(
             return t
 
         x_sc = sb("x_sc", [P, GROUPS, M], U8)
-        a_sc = sb("a_sc", [P, GROUPS, N], U8)
-        b_sc = sb("b_sc", [P, GROUPS, N], U8)
+        a_sc = [sb("a_sc0", [P, GROUPS, WIDE], U8), sb("a_sc1", [P, GROUPS, N - WIDE], U8)]
+        b_sc = [sb("b_sc0", [P, GROUPS, WIDE], U8), sb("b_sc1", [P, GROUPS, N - WIDE], U8)]
         x_w = [sb("x_w%d" % g, [P, M], U32) for g in range(GROUPS)]
         a_w = [sb("a_w%d" % j, [P, GROUPS, 2 * WIDE], U8) for j in range(CHUNKS)]
         b_w = [sb("b_w%d" % j, [P, GROUPS, WIDE], U32) for j in range(CHUNKS)]
@@ -69,16 +71,17 @@ def tile_uniformity_pair_weights_k3_kernel(
         def zero(t):
             nc.vector.memset(t.bitcast(I32), 0)
 
-        def load_scales(plane, rows, r):
-            src = rows.rearrange("g (q r) n -> r q g n", r=4)[r]
-            nc.sync.dma_start(out=plane[r:P:32, :, :].bitcast(I32), in_=src.bitcast(I32))
+        def load_scales(eng, plane, first_row, rows, lo, hi):
+            for r in range(4):
+                src = rows.rearrange("g (q r) n -> r q g n", r=4)[r][:, :, lo:hi]
+                eng.dma_start(out=plane[first_row + r : P : 32, :, :].bitcast(I32), in_=src.bitcast(I32))
 
         def load_x(eng, g):
             eng.dma_start(out=x_w[g][:].bitcast(I32), in_=x_words[g].rearrange("p m t -> p (m t)").bitcast(I32))
 
-        def load_a(eng, j):
-            src = a_words.rearrange("g p n -> p g n")[:, :, 2 * WIDE * j : 2 * WIDE * (j + 1)]
-            eng.dma_start(out=a_w[j][:].bitcast(I32), in_=src.bitcast(I32))
+        def load_a(j, g_lo, g_hi):
+            src = a_words.rearrange("g p n -> p g n")[:, g_lo:g_hi, 2 * WIDE * j : 2 * WIDE * (j + 1)]
+            nc.sync.dma_start(out=a_w[j][:, g_lo:g_hi, :].bitcast(I32), in_=src.bitcast(I32))
 
         def load_b(j):
             src = b_words.rearrange("g p n t -> p g (n t)")[:, :, PACK * WIDE * j : PACK * WIDE * (j + 1)]
@@ -89,16 +92,14 @@ def tile_uniformity_pair_weights_k3_kernel(
             nc.sync.dma_start(out=c_raw[j, g][:], in_=src.rearrange("(p t) n -> p t n", t=PACK))
 
         def weave(j, g, lo, hi):
-            dst = c_grp[j, g][:, lo:hi, :].rearrange("p (n i) t -> p n t i", i=4)
-            src = c_raw[j, g][:, :, lo:hi].rearrange("p t (n i) -> p n t i", i=4)
-            return dst, src
+            return c_grp[j, g][:, lo:hi, :], c_raw[j, g][:, :, lo:hi].rearrange("p t n -> p n t")
 
         def weave_v(j, g):
             dst, src = weave(j, g, 0, C_SPLIT)
             nc.vector.tensor_copy(out=dst, in_=src)
 
-        def weave_s(j, g):
-            dst, src = weave(j, g, C_SPLIT, WIDE)
+        def weave_s(j, g, lo=C_SPLIT):
+            dst, src = weave(j, g, lo, WIDE)
             nc.scalar.copy(out=dst, in_=src)
 
         def quant_c(j, g):
@@ -113,16 +114,17 @@ def tile_uniformity_pair_weights_k3_kernel(
         def mx(i, which, g):
             j, mt = divmod(i, ROWS)
             ms = slice(P * mt, P * (mt + 1))
-            ns = slice(WIDE * j, WIDE * (j + 1))
+            part = min(j, 1)
+            ns = slice(WIDE * (j - part), WIDE * (j - part + 1))
             if which == "a":
-                rhs, rhs_sc = a_w[j][:, g, :].bitcast(FP4X4), a_sc[:, g, ns]
+                rhs, rhs_sc = a_w[j][:, g, :].bitcast(FP4X4), a_sc[part][:, g, ns]
             elif which == "b":
-                rhs, rhs_sc = b_w[j][:, g, :].bitcast(FP8X4), b_sc[:, g, ns]
+                rhs, rhs_sc = b_w[j][:, g, :].bitcast(FP8X4), b_sc[part][B_ROW:P, g, ns]
             else:
                 rhs, rhs_sc = c_w[j, g][:].bitcast(FP8X4), c_sc[j, g][:]
             first = which == "a" and g == 0
             if first:
-                acc[i] = bank(i if i < 8 else MX_RING[(i - 6) % len(MX_RING)], [P, WIDE])
+                acc[i] = bank(MX_BANK[i], [P, WIDE])
             nc.tensor.matmul_mx(
                 out=acc[i][:],
                 lhsT=x_w[g][:, ms].bitcast(FP8X4),
@@ -133,26 +135,33 @@ def tile_uniformity_pair_weights_k3_kernel(
                 stop=(which == "c" and g == GROUPS - 1),
             )
 
-        def mx_tile(i):
-            for which in "abc":
+        def mx_parts(i, parts):
+            for which in parts:
                 for g in range(GROUPS):
                     mx(i, which, g)
 
-        def exp(i):
-            nc.scalar.activation(out=e_t[i][:], in_=acc[i][:], func=ACT.Exp)
+        def exp(i, lo=0, hi=WIDE):
+            nc.scalar.activation(out=e_t[i][:, lo:hi], in_=acc[i][:, lo:hi], func=ACT.Exp)
 
-        def mul(i):
+        def mul(i, lo=0, hi=WIDE):
             j, mt = divmod(i, ROWS)
             nc.vector.tensor_tensor(
-                out=y_t[i][:], in0=e_t[i][:], in1=gain_all[:, WIDE * j : WIDE * (j + 1)], op=ALU.mult
+                out=y_t[i][:, lo:hi], in0=e_t[i][:, lo:hi], in1=gain_all[:, WIDE * j + lo : WIDE * j + hi], op=ALU.mult
             )
-            nc.sync.dma_start(out=out_0[P * mt : P * (mt + 1), WIDE * j : WIDE * (j + 1)], in_=y_t[i][:])
+            if hi == WIDE:
+                nc.sync.dma_start(out=out_0[P * mt : P * (mt + 1), WIDE * j : WIDE * (j + 1)], in_=y_t[i][:])
 
-        def cast(i):
-            nc.vector.tensor_copy(
-                out=y_bf[i][:].rearrange("m (u p e) -> m u p e", u=2, e=2),
-                in_=y_t[i][:].rearrange("m (p u e) -> m u p e", u=2, e=2),
-            )
+        def cast_views(i, lo, hi):
+            dst = y_bf[i][:].rearrange("m (u p e) -> m u p e", u=2, e=2)[:, :, lo // PACK : hi // PACK, :]
+            return dst, y_t[i][:, lo:hi].rearrange("m (p u e) -> m u p e", u=2, e=2)
+
+        def cast(i, lo=0, hi=WIDE):
+            dst, src = cast_views(i, lo, hi)
+            nc.vector.tensor_copy(out=dst, in_=src)
+
+        def cast_s(i):
+            dst, src = cast_views(i, 0, WIDE)
+            nc.scalar.copy(out=dst, in_=src)
 
         turned = {}
 
@@ -186,33 +195,35 @@ def tile_uniformity_pair_weights_k3_kernel(
             dst = out_2.rearrange("g (q r) m -> r q g m", r=4)[r]
             eng.dma_start(out=dst[:, lo:hi, :].bitcast(I32), in_=y_sc[r:P:32, lo:hi, :].bitcast(I32))
 
+        load_a(0, 0, 1)
         nc.vector.memset(zeros[:], 0.0)
-        zero(x_sc[:])
         nc.vector.memset(gain_row[:], 0.0)
-        zero(a_sc[:])
-        zero(b_sc[:])
+        zero(x_sc[:])
+        zero(a_sc[0][:])
+        zero(b_sc[0][:])
+        zero(a_sc[1][:])
+        zero(b_sc[1][:])
         nc.scalar.activation(out=ones[:], in_=zeros[:], func=ACT.Exp)
-        load_x(nc.gpsimd, 0)
-        load_a(nc.gpsimd, 0)
-        make_identity(nc, ident[:])
-        for r in range(4):
-            load_scales(x_sc, x_scales, r)
         nc.sync.dma_start(out=gain_row[0:1, :], in_=gain.rearrange("(o n) -> o n", o=1))
-        for r in range(4):
-            load_scales(a_sc, a_scales, r)
+        load_scales(nc.sync, x_sc, 0, x_scales, 0, M)
+        load_x(nc.sync, 0)
+        load_scales(nc.sync, a_sc[0], 0, a_scales, 0, WIDE)
+        load_a(0, 1, 2)
         load_x(nc.sync, 1)
         load_b(0)
-        for r in range(4):
-            load_scales(b_sc, b_scales, r)
+        load_scales(nc.sync, b_sc[0], B_ROW, b_scales, 0, WIDE)
         load_c(0, 0)
+        make_identity(nc, ident[:])
+        load_scales(nc.gpsimd, a_sc[1], 0, a_scales, WIDE, N)
+        load_scales(nc.gpsimd, b_sc[1], B_ROW, b_scales, WIDE, N)
         load_c(0, 1)
         load_c(1, 0)
-        load_c(1, 1)
-        load_a(nc.sync, 1)
+        load_a(1, 0, 2)
         load_b(1)
+        load_c(1, 1)
         load_c(2, 0)
         load_c(2, 1)
-        load_a(nc.sync, 2)
+        load_a(2, 0, 2)
         load_b(2)
 
         for j in range(CHUNKS):
@@ -221,89 +232,116 @@ def tile_uniformity_pair_weights_k3_kernel(
             nc.tensor.matmul(spread[:], lhsT=ones[:], rhs=gain_row[:, ns], start=True, stop=True)
             nc.scalar.copy(out=gain_all[:, ns], in_=spread[:])
 
-        for j in range(2):
-            for g in range(GROUPS):
-                weave_s(j, g)
-                weave_v(j, g)
-                quant_c(j, g)
+        for j, g in [(0, 0), (0, 1), (1, 0)]:
+            weave_s(j, g)
+            weave_v(j, g)
+            quant_c(j, g)
 
         for which in "abc":
             for g in range(GROUPS):
                 for i in range(ROWS):
                     mx(i, which, g)
-        for i in range(ROWS):
+        for i in range(4):
             exp(i)
+        mul(0)
+        mul(1)
+        cast(0)
+        weave_s(1, 1)
+        weave_v(1, 1)
+        mul(2)
+        quant_c(1, 1)
+        cast(1)
+        exp(4)
+        exp(5)
+        for i in range(3, ROWS):
             mul(i)
-            if i > 0:
-                cast(i - 1)
+            cast(i - 1)
 
-        mx_tile(6)
+        for i in range(6, 9):
+            mx_parts(i, "ab")
         weave_s(2, 0)
+        for i in range(6, 9):
+            mx_parts(i, "c")
+            exp(i)
         weave_v(2, 0)
         cast(5)
         quant_c(2, 0)
-        exp(6)
         mul(6)
-        weave_s(2, 1)
-        weave_v(2, 1)
+        weave_s(2, 1, 0)
+        mul(7)
         cast(6)
+        mx_parts(9, "abc")
+        exp(9)
+        mul(8)
         quant_c(2, 1)
-        for i in range(7, 11):
-            mx_tile(i)
-            exp(i)
-            mul(i)
-            if i > 7:
-                cast(i - 1)
+        cast(7)
+        mx_parts(10, "abc")
+        exp(10)
+        mul(9)
+        cast(8)
+        mx_parts(11, "abc")
+        exp(11)
+        mul(10)
+        cast(9)
         for s in range(3):
             turn(2 * s, 2, 3 + s)
         for s in range(3):
             evac(2 * s, 2)
-        quant_y(0, 2)
-        cast(10)
-        quant_y(2, 2)
-        mx_tile(11)
-        exp(11)
         mul(11)
-        quant_y(4, 2)
-        store_words(0, 0, M)
+        cast(10)
+        quant_y(0, 2)
         cast(11)
+        quant_y(2, 2)
 
-        mx_tile(12)
+        mx_parts(12, "abc")
         exp(12)
         mul(12)
-        mx_tile(13)
+        quant_y(4, 2)
+        store_words(0, 0, M)
+        mx_parts(13, "abc")
         exp(13)
         mul(13)
         cast(12)
-        for s in range(3):
-            turn(6 + 2 * s, 2, 3 + s)
-        for s in range(3):
-            evac(6 + 2 * s, 2)
-        quant_y(6, 2)
         cast(13)
-        quant_y(8, 2)
-        mx_tile(14)
+        mx_parts(14, "abc")
         exp(14)
         mul(14)
+        mx_parts(15, "abc")
+        exp(15)
+        mul(15)
+        cast(14)
+        for s in range(4):
+            turn(6 + 2 * s, 2, 2 + s)
+        evac(6, 2)
+        evac(8, 2)
+        quant_y(6, 2)
+        cast(15)
+        quant_y(8, 2)
+        evac(10, 2)
+        evac(12, 2)
+        mx_parts(16, "abc")
+        exp(16)
         quant_y(10, 2)
         store_words(1, 0, M)
         for r in range(4):
             store_scales(nc.sync, r, 0, 2)
-        cast(14)
-        for i in range(15, 18):
-            mx_tile(i)
-            exp(i)
-            mul(i)
-            cast(i)
-        turn(12, 2, 3)
-        turn(14, 2, 4)
-        turn(16, 1, 5)
-        turn(17, 1, 2)
-        evac(12, 2)
+        quant_y(12, 2)
+        mul(16)
+        cast(16)
+        mx_parts(17, "abc")
+        half = WIDE // 2
+        exp(17, 0, half)
+        exp(17, half, WIDE)
+        mul(17, 0, half)
+        mul(17, half, WIDE)
+        cast(17, 0, half)
+        cast(17, half, WIDE)
+        turn(14, 2, 2)
+        turn(16, 1, 3)
+        turn(17, 1, 4)
         evac(14, 2)
         evac(16, 1)
         evac(17, 1)
-        quant_y(12, 2)
         quant_y(14, 2)
         store_words(2, 0, 4 * P)
         quant_y(16, 1)
@@ -313,6 +351,3 @@ def tile_uniformity_pair_weights_k3_kernel(
         store_scales(nc.sync, 1, 2, 3)
         store_scales(nc.scalar, 2, 2, 3)
         store_scales(nc.sync, 3, 2, 3)
-
-
-MX_RING = [6, 7, 0, 1, 2]

@@ -94,8 +94,8 @@ def tile_uniformity_pair_weights_k3_kernel(
         def weave(j, g, lo, hi):
             return c_grp[j, g][:, lo:hi, :], c_raw[j, g][:, :, lo:hi].rearrange("p t n -> p n t")
 
-        def weave_v(j, g):
-            dst, src = weave(j, g, 0, C_SPLIT)
+        def weave_v(j, g, hi=C_SPLIT):
+            dst, src = weave(j, g, 0, hi)
             nc.vector.tensor_copy(out=dst, in_=src)
 
         def weave_s(j, g, lo=C_SPLIT):
@@ -111,22 +111,22 @@ def tile_uniformity_pair_weights_k3_kernel(
 
         acc = {}
 
-        def mx(i, which, g):
+        def mx(i, which, g, lo=0, hi=WIDE, b=None):
             j, mt = divmod(i, ROWS)
             ms = slice(P * mt, P * (mt + 1))
             part = min(j, 1)
-            ns = slice(WIDE * (j - part), WIDE * (j - part + 1))
+            ns = slice(WIDE * (j - part) + lo, WIDE * (j - part) + hi)
             if which == "a":
-                rhs, rhs_sc = a_w[j][:, g, :].bitcast(FP4X4), a_sc[part][:, g, ns]
+                rhs, rhs_sc = a_w[j][:, g, 2 * lo : 2 * hi].bitcast(FP4X4), a_sc[part][:, g, ns]
             elif which == "b":
-                rhs, rhs_sc = b_w[j][:, g, :].bitcast(FP8X4), b_sc[part][B_ROW:P, g, ns]
+                rhs, rhs_sc = b_w[j][:, g, lo:hi].bitcast(FP8X4), b_sc[part][B_ROW:P, g, ns]
             else:
-                rhs, rhs_sc = c_w[j, g][:].bitcast(FP8X4), c_sc[j, g][:]
+                rhs, rhs_sc = c_w[j, g][:, lo:hi].bitcast(FP8X4), c_sc[j, g][:, lo:hi]
             first = which == "a" and g == 0
             if first:
-                acc[i] = bank(MX_BANK[i], [P, WIDE])
+                acc[i, lo] = bank(MX_BANK[i] if b is None else b, [P, hi - lo])
             nc.tensor.matmul_mx(
-                out=acc[i][:],
+                out=acc[i, lo][:],
                 lhsT=x_w[g][:, ms].bitcast(FP8X4),
                 lhsT_scale=x_sc[:, g, ms],
                 rhs=rhs,
@@ -135,13 +135,13 @@ def tile_uniformity_pair_weights_k3_kernel(
                 stop=(which == "c" and g == GROUPS - 1),
             )
 
-        def mx_parts(i, parts):
-            for which in parts:
-                for g in range(GROUPS):
-                    mx(i, which, g)
+        def mx_parts(i, parts, lo=0, hi=WIDE, b=None):
+            for g in range(GROUPS):
+                for which in parts:
+                    mx(i, which, g, lo, hi, b)
 
         def exp(i, lo=0, hi=WIDE):
-            nc.scalar.activation(out=e_t[i][:, lo:hi], in_=acc[i][:, lo:hi], func=ACT.Exp)
+            nc.scalar.activation(out=e_t[i][:, lo:hi], in_=acc[i, lo][:], func=ACT.Exp)
 
         def mul(i, lo=0, hi=WIDE):
             j, mt = divmod(i, ROWS)
@@ -214,9 +214,9 @@ def tile_uniformity_pair_weights_k3_kernel(
         load_scales(nc.sync, b_sc[0], B_ROW, b_scales, 0, WIDE)
         load_c(0, 0)
         make_identity(nc, ident[:])
-        load_scales(nc.gpsimd, a_sc[1], 0, a_scales, WIDE, N)
-        load_scales(nc.gpsimd, b_sc[1], B_ROW, b_scales, WIDE, N)
         load_c(0, 1)
+        load_scales(nc.sync, a_sc[1], 0, a_scales, WIDE, N)
+        load_scales(nc.sync, b_sc[1], B_ROW, b_scales, WIDE, N)
         load_c(1, 0)
         load_a(1, 0, 2)
         load_b(1)
@@ -233,8 +233,8 @@ def tile_uniformity_pair_weights_k3_kernel(
             nc.scalar.copy(out=gain_all[:, ns], in_=spread[:])
 
         for j, g in [(0, 0), (0, 1), (1, 0)]:
-            weave_s(j, g)
-            weave_v(j, g)
+            weave_s(j, g, 320)
+            weave_v(j, g, 320)
             quant_c(j, g)
 
         for which in "abc":
@@ -327,26 +327,25 @@ def tile_uniformity_pair_weights_k3_kernel(
             store_scales(nc.sync, r, 0, 2)
         quant_y(12, 2)
         mul(16)
-        cast(16)
-        mx_parts(17, "abc")
-        half = WIDE // 2
-        exp(17, 0, half)
-        exp(17, half, WIDE)
-        mul(17, 0, half)
-        mul(17, half, WIDE)
-        cast(17, 0, half)
-        cast(17, half, WIDE)
-        turn(14, 2, 2)
-        turn(16, 1, 3)
-        turn(17, 1, 4)
+        for q in range(4):
+            mx_parts(17, "abc", P * q, P * (q + 1), q)
+            exp(17, P * q, P * (q + 1))
+            mul(17, P * q, P * (q + 1))
+            if q == 0:
+                cast(16)
+        cast(17, 0, 3 * P)
+        cast(17, 3 * P, WIDE)
+        turn(14, 2, 4)
+        turn(16, 1, 5)
+        turn(17, 1, 6)
         evac(14, 2)
         evac(16, 1)
         evac(17, 1)
         quant_y(14, 2)
-        store_words(2, 0, 4 * P)
         quant_y(16, 1)
+        store_words(2, 0, 5 * P)
         quant_y(17, 1)
-        store_words(2, 4 * P, M)
+        store_words(2, 5 * P, M)
         store_scales(nc.scalar, 0, 2, 3)
         store_scales(nc.sync, 1, 2, 3)
         store_scales(nc.scalar, 2, 2, 3)

@@ -61,9 +61,10 @@ def tile_uniformity_pair_weights_k3_kernel(
         gain_row = sb("gain_row", [P, N], BF16)
         gain_all = sb("gain_all", [P, N], F32)
         ident = sb("ident", [P, P], F32)
-        e_t = [sb("e%d" % i, [P, WIDE], F32) for i in range(TILES)]
-        y_t = [sb("y%d" % i, [P, WIDE], F32) for i in range(TILES)]
-        y_bf = [sb("ybf%d" % i, [P, WIDE], BF16) for i in range(TILES)]
+        e_t = [sb("e%d" % h, [P, 2, WIDE], F32) for h in range(TILES // 2)]
+        y_t = [sb("y%d" % h, [P, 2, WIDE], F32) for h in range(TILES // 2)]
+        y_bf = [sb("ybf%d" % h, [P, 2, 2, WIDE // 2], BF16) for h in range(TILES // 2 - 1)]
+        last_bf = [sb("last_bf%d" % s, [P, 2, WIDE // 2], BF16) for s in range(2)]
         y_grp = [sb("ygrp%d" % j, [P, M * PACK], BF16) for j in range(CHUNKS)]
         y_w = [sb("y_w%d" % j, [P, M], U32) for j in range(CHUNKS)]
         y_sc = sb("y_sc", [P, CHUNKS, M], U8)
@@ -141,43 +142,60 @@ def tile_uniformity_pair_weights_k3_kernel(
                     mx(i, which, g, lo, hi, b)
 
         def exp(i, lo=0, hi=WIDE):
-            nc.scalar.activation(out=e_t[i][:, lo:hi], in_=acc[i, lo][:], func=ACT.Exp)
+            nc.scalar.activation(out=e_t[i // 2][:, i % 2, lo:hi], in_=acc[i, lo][:], func=ACT.Exp)
+
+        def store_y(i):
+            j, mt = divmod(i, ROWS)
+            nc.sync.dma_start(out=out_0[P * mt : P * (mt + 1), WIDE * j : WIDE * (j + 1)], in_=y_t[i // 2][:, i % 2, :])
+
+        def mul_pair(i):
+            j = i // ROWS
+            gains = gain_all[:, WIDE * j : WIDE * (j + 1)].unsqueeze(1).to_broadcast([P, 2, WIDE])
+            nc.vector.tensor_tensor(out=y_t[i // 2][:], in0=e_t[i // 2][:], in1=gains, op=ALU.mult)
+            store_y(i)
+            store_y(i + 1)
 
         def mul(i, lo=0, hi=WIDE):
-            j, mt = divmod(i, ROWS)
+            j = i // ROWS
             nc.vector.tensor_tensor(
-                out=y_t[i][:, lo:hi], in0=e_t[i][:, lo:hi], in1=gain_all[:, WIDE * j + lo : WIDE * j + hi], op=ALU.mult
+                out=y_t[i // 2][:, i % 2, lo:hi],
+                in0=e_t[i // 2][:, i % 2, lo:hi],
+                in1=gain_all[:, WIDE * j + lo : WIDE * j + hi],
+                op=ALU.mult,
             )
             if hi == WIDE:
-                nc.sync.dma_start(out=out_0[P * mt : P * (mt + 1), WIDE * j : WIDE * (j + 1)], in_=y_t[i][:])
+                store_y(i)
 
-        def cast_views(i, lo, hi):
-            dst = y_bf[i][:].rearrange("m (u p e) -> m u p e", u=2, e=2)[:, :, lo // PACK : hi // PACK, :]
-            return dst, y_t[i][:, lo:hi].rearrange("m (p u e) -> m u p e", u=2, e=2)
+        def cast_pair(i, copy=nc.vector.tensor_copy):
+            copy(
+                out=y_bf[i // 2][:].rearrange("m u s (p e) -> m u (s p) e", e=2),
+                in_=y_t[i // 2][:].rearrange("m s (p u e) -> m u (s p) e", u=2, e=2),
+            )
+
+        def bf_tile(i):
+            return last_bf[i % 2] if i >= TILES - 2 else y_bf[i // 2][:, :, i % 2, :]
 
         def cast(i, lo=0, hi=WIDE):
-            dst, src = cast_views(i, lo, hi)
-            nc.vector.tensor_copy(out=dst, in_=src)
-
-        def cast_s(i):
-            dst, src = cast_views(i, 0, WIDE)
-            nc.scalar.copy(out=dst, in_=src)
+            nc.vector.tensor_copy(
+                out=bf_tile(i)[:, :, lo // 2 : hi // 2].rearrange("m u (p e) -> m u p e", e=2),
+                in_=y_t[i // 2][:, i % 2, lo:hi].rearrange("m (p u e) -> m u p e", u=2, e=2),
+            )
 
         turned = {}
 
         def turn(i, count, b):
             turned[i] = bank(b, [P, count, 2, P])
             for s in range(count):
-                words = y_bf[i + s][:].bitcast(F32)
                 for u in range(2):
-                    nc.tensor.transpose(turned[i][:, s, u, :], words[:, P * u : P * (u + 1)], ident[:])
+                    words = bf_tile(i + s)[:, u, :].bitcast(F32)
+                    nc.tensor.transpose(turned[i][:, s, u, :], words, ident[:])
 
         def grp_cols(i, count):
             mt = i % ROWS
             return y_grp[i // ROWS][:, P * PACK * mt : P * PACK * (mt + count)]
 
-        def evac(i, count):
-            nc.scalar.copy(
+        def evac(i, count, copy=nc.scalar.copy):
+            copy(
                 out=grp_cols(i, count).bitcast(F32).rearrange("p (s m u) -> p s m u", s=count, u=2),
                 in_=turned[i][:].rearrange("p s u m -> p s m u"),
             )
@@ -196,13 +214,14 @@ def tile_uniformity_pair_weights_k3_kernel(
             eng.dma_start(out=dst[:, lo:hi, :].bitcast(I32), in_=y_sc[r:P:32, lo:hi, :].bitcast(I32))
 
         load_a(0, 0, 1)
-        nc.vector.memset(zeros[:], 0.0)
-        nc.vector.memset(gain_row[:], 0.0)
+        zero(gain_row[:])
+        zero(zeros[:])
         zero(x_sc[:])
         zero(a_sc[0][:])
         zero(b_sc[0][:])
         zero(a_sc[1][:])
         zero(b_sc[1][:])
+        zero(ident[:])
         nc.scalar.activation(out=ones[:], in_=zeros[:], func=ACT.Exp)
         nc.sync.dma_start(out=gain_row[0:1, :], in_=gain.rearrange("(o n) -> o n", o=1))
         load_scales(nc.sync, x_sc, 0, x_scales, 0, M)
@@ -213,9 +232,9 @@ def tile_uniformity_pair_weights_k3_kernel(
         load_b(0)
         load_scales(nc.sync, b_sc[0], B_ROW, b_scales, 0, WIDE)
         load_c(0, 0)
-        make_identity(nc, ident[:])
+        make_identity(nc, ident[:], nomemset=True)
         load_c(0, 1)
-        load_scales(nc.sync, a_sc[1], 0, a_scales, WIDE, N)
+        load_scales(nc.gpsimd, a_sc[1], 0, a_scales, WIDE, N)
         load_scales(nc.sync, b_sc[1], B_ROW, b_scales, WIDE, N)
         load_c(1, 0)
         load_a(1, 0, 2)
@@ -243,109 +262,96 @@ def tile_uniformity_pair_weights_k3_kernel(
                     mx(i, which, g)
         for i in range(4):
             exp(i)
-        mul(0)
-        mul(1)
-        cast(0)
+        mul_pair(0)
         weave_s(1, 1)
         weave_v(1, 1)
-        mul(2)
+        cast_pair(0)
         quant_c(1, 1)
-        cast(1)
+        mul_pair(2)
         exp(4)
         exp(5)
-        for i in range(3, ROWS):
-            mul(i)
-            cast(i - 1)
 
         for i in range(6, 9):
             mx_parts(i, "ab")
         weave_s(2, 0)
+        mul_pair(4)
+        cast_pair(2)
+        weave_v(2, 0)
+        cast_pair(4)
+        quant_c(2, 0)
         for i in range(6, 9):
             mx_parts(i, "c")
             exp(i)
-        weave_v(2, 0)
-        cast(5)
-        quant_c(2, 0)
-        mul(6)
+        mul_pair(6)
         weave_s(2, 1, 0)
-        mul(7)
-        cast(6)
         mx_parts(9, "abc")
         exp(9)
-        mul(8)
         quant_c(2, 1)
-        cast(7)
+        cast_pair(6)
+        mul_pair(8)
         mx_parts(10, "abc")
         exp(10)
-        mul(9)
-        cast(8)
         mx_parts(11, "abc")
         exp(11)
-        mul(10)
-        cast(9)
         for s in range(3):
             turn(2 * s, 2, 3 + s)
         for s in range(3):
             evac(2 * s, 2)
-        mul(11)
-        cast(10)
-        quant_y(0, 2)
-        cast(11)
-        quant_y(2, 2)
+        mul_pair(10)
+        cast_pair(8)
+        quant_y(0, 4)
+        quant_y(4, 2)
+        store_words(0, 0, M)
 
         mx_parts(12, "abc")
         exp(12)
-        mul(12)
-        quant_y(4, 2)
-        store_words(0, 0, M)
+        cast_pair(10, nc.scalar.copy)
         mx_parts(13, "abc")
         exp(13)
-        mul(13)
-        cast(12)
-        cast(13)
+        mul_pair(12)
         mx_parts(14, "abc")
         exp(14)
+        for s in range(3):
+            turn(6 + 2 * s, 2, 3 + s)
         mul(14)
+        cast_pair(12)
+        for s in range(3):
+            evac(6 + 2 * s, 2)
         mx_parts(15, "abc")
         exp(15)
-        mul(15)
+        quant_y(6, 4)
         cast(14)
-        for s in range(4):
-            turn(6 + 2 * s, 2, 2 + s)
-        evac(6, 2)
-        evac(8, 2)
-        quant_y(6, 2)
-        cast(15)
-        quant_y(8, 2)
-        evac(10, 2)
-        evac(12, 2)
-        mx_parts(16, "abc")
-        exp(16)
         quant_y(10, 2)
         store_words(1, 0, M)
         for r in range(4):
             store_scales(nc.sync, r, 0, 2)
-        quant_y(12, 2)
+        mul(15)
+        mx_parts(16, "abc")
+        exp(16)
+        cast(15)
         mul(16)
         for q in range(4):
             mx_parts(17, "abc", P * q, P * (q + 1), q)
             exp(17, P * q, P * (q + 1))
-            mul(17, P * q, P * (q + 1))
-            if q == 0:
-                cast(16)
-        cast(17, 0, 3 * P)
-        cast(17, 3 * P, WIDE)
-        turn(14, 2, 4)
-        turn(16, 1, 5)
-        turn(17, 1, 6)
+        mul(17, 0, 2 * P)
+        cast(16)
+        mul(17, 2 * P, WIDE)
+        cast(17, 0, 2 * P)
+        cast(17, 2 * P, WIDE)
+        turn(12, 2, 4)
+        turn(14, 2, 5)
+        turn(16, 1, 6)
+        turn(17, 1, 7)
+        evac(12, 2)
         evac(14, 2)
-        evac(16, 1)
+        evac(16, 1, nc.vector.tensor_copy)
         evac(17, 1)
+        quant_y(12, 2)
+        store_words(2, 0, 2 * P)
         quant_y(14, 2)
-        quant_y(16, 1)
-        store_words(2, 0, 5 * P)
-        quant_y(17, 1)
-        store_words(2, 5 * P, M)
+        store_words(2, 2 * P, 4 * P)
+        quant_y(16, 2)
+        store_words(2, 4 * P, M)
         store_scales(nc.scalar, 0, 2, 3)
         store_scales(nc.sync, 1, 2, 3)
         store_scales(nc.scalar, 2, 2, 3)

from contextlib import ExitStack

import concourse.mybir as mybir
from concourse.masks import make_identity

M, K, N = 768, 1024, 1536
FLOPS = 3 * 2 * M * K * N

F32 = mybir.dt.float32
BF16 = mybir.dt.bfloat16
I32 = mybir.dt.int32
U32 = mybir.dt.uint32
U8 = mybir.dt.uint8
FP8X4 = mybir.dt.float8_e4m3fn_x4
FP4X4 = mybir.dt.float4_e2m1fn_x4
ACT = mybir.ActivationFunctionType
ALU = mybir.AluOpType

P = 128
PACK = 4
GROUPS = K // (P * PACK)
WIDE = 512
CHUNKS = N // WIDE
ROWS = M // P
TILES = CHUNKS * ROWS
B_ROW = 4
MX_BANK = [0, 1, 2, 3, 4, 5, 6, 7, 0, 1, 2, 6, 7, 0, 1, 6, 7, 0]
C_SPLIT = 256


def tile_uniformity_pair_weights_k3_kernel(
    tc, x_words, x_scales, a_words, a_scales, b_words, b_scales, c, gain, out_0, out_1, out_2
):
    nc = tc.nc
    with ExitStack() as ctx:
        keep = ctx.enter_context(tc.tile_pool(name="keep", bufs=1))
        psum = ctx.enter_context(tc.psum_pool(name="psum", bufs=1))
        ctx.enter_context(tc.manual_schedule())

        def sb(name, shape, dtype):
            t = keep.tile(shape, dtype, name=name, tag=name, align_bytes=64)
            return t

        def bank(i, shape):
            t = psum.tile(shape, F32, name="bank%d" % i, tag="bank%d" % i)
            return t

        x_sc = sb("x_sc", [P, GROUPS, M], U8)
        a_sc = [sb("a_sc0", [P, GROUPS, WIDE], U8), sb("a_sc1", [P, GROUPS, N - WIDE], U8)]
        b_sc = [sb("b_sc0", [P, GROUPS, WIDE], U8), sb("b_sc1", [P, GROUPS, N - WIDE], U8)]
        x_w = [sb("x_w%d" % g, [P, M], U32) for g in range(GROUPS)]
        a_w = [sb("a_w%d" % j, [P, GROUPS, 2 * WIDE], U8) for j in range(CHUNKS)]
        b_w = [sb("b_w%d" % j, [P, GROUPS, WIDE], U32) for j in range(CHUNKS)]
        pieces = [(j, g) for j in range(CHUNKS) for g in range(GROUPS)]
        c_raw = {k: sb("c_raw%d%d" % k, [P, PACK, WIDE], BF16) for k in pieces}
        c_grp = {k: sb("c_grp%d%d" % k, [P, WIDE, PACK], BF16) for k in pieces}
        c_w = {k: sb("c_w%d%d" % k, [P, WIDE], U32) for k in pieces}
        c_sc = {k: sb("c_sc%d%d" % k, [P, WIDE], U8) for k in pieces}
        zeros = sb("zeros", [P, P], BF16)
        ones = sb("ones", [P, P], BF16)
        gain_row = sb("gain_row", [P, N], BF16)
        gain_all = sb("gain_all", [P, N], F32)
        ident = sb("ident", [P, P], F32)
        e_t = [sb("e%d" % h, [P, 2, WIDE], F32) for h in range(TILES // 2)]
        y_t = [sb("y%d" % h, [P, 2, WIDE], F32) for h in range(TILES // 2)]
        y_bf = [sb("ybf%d" % h, [P, 2, 2, WIDE // 2], BF16) for h in range(TILES // 2 - 1)]
        last_bf = [sb("last_bf%d" % s, [P, 2, WIDE // 2], BF16) for s in range(2)]
        y_grp = [sb("ygrp%d" % j, [P, M * PACK], BF16) for j in range(CHUNKS)]
        y_w = [sb("y_w%d" % j, [P, M], U32) for j in range(CHUNKS)]
        y_sc = sb("y_sc", [P, CHUNKS, M], U8)

        def zero(t):
            nc.vector.memset(t.bitcast(I32), 0)

        def load_scales(eng, plane, first_row, rows, lo, hi):
            for r in range(4):
                src = rows.rearrange("g (q r) n -> r q g n", r=4)[r][:, :, lo:hi]
                eng.dma_start(out=plane[first_row + r : P : 32, :, :].bitcast(I32), in_=src.bitcast(I32))

        def load_x(eng, g):
            eng.dma_start(out=x_w[g][:].bitcast(I32), in_=x_words[g].rearrange("p m t -> p (m t)").bitcast(I32))

        def load_a(j, g_lo, g_hi):
            src = a_words.rearrange("g p n -> p g n")[:, g_lo:g_hi, 2 * WIDE * j : 2 * WIDE * (j + 1)]
            nc.sync.dma_start(out=a_w[j][:, g_lo:g_hi, :].bitcast(I32), in_=src.bitcast(I32))

        def load_b(j):
            src = b_words.rearrange("g p n t -> p g (n t)")[:, :, PACK * WIDE * j : PACK * WIDE * (j + 1)]
            nc.sync.dma_start(out=b_w[j][:].bitcast(I32), in_=src.bitcast(I32))

        def load_c(j, g):
            src = c[P * PACK * g : P * PACK * (g + 1), WIDE * j : WIDE * (j + 1)]
            nc.sync.dma_start(out=c_raw[j, g][:], in_=src.rearrange("(p t) n -> p t n", t=PACK))

        def weave(j, g, lo, hi):
            return c_grp[j, g][:, lo:hi, :], c_raw[j, g][:, :, lo:hi].rearrange("p t n -> p n t")

        def weave_v(j, g, hi=C_SPLIT):
            dst, src = weave(j, g, 0, hi)
            nc.vector.tensor_copy(out=dst, in_=src)

        def weave_s(j, g, lo=C_SPLIT):
            dst, src = weave(j, g, lo, WIDE)
            nc.scalar.copy(out=dst, in_=src)

        def quant_c(j, g):
            nc.vector.quantize_mx(
                out=c_w[j, g][:].bitcast(FP8X4),
                scales=c_sc[j, g][:],
                in_=c_grp[j, g][:].rearrange("p n t -> p (n t)"),
            )

        acc = {}

        def mx(i, which, g, lo=0, hi=WIDE, b=None):
            j, mt = divmod(i, ROWS)
            ms = slice(P * mt, P * (mt + 1))
            part = min(j, 1)
            ns = slice(WIDE * (j - part) + lo, WIDE * (j - part) + hi)
            if which == "a":
                rhs, rhs_sc = a_w[j][:, g, 2 * lo : 2 * hi].bitcast(FP4X4), a_sc[part][:, g, ns]
            elif which == "b":
                rhs, rhs_sc = b_w[j][:, g, lo:hi].bitcast(FP8X4), b_sc[part][B_ROW:P, g, ns]
            else:
                rhs, rhs_sc = c_w[j, g][:, lo:hi].bitcast(FP8X4), c_sc[j, g][:, lo:hi]
            first = which == "a" and g == 0
            if first:
                acc[i, lo] = bank(MX_BANK[i] if b is None else b, [P, hi - lo])
            nc.tensor.matmul_mx(
                out=acc[i, lo][:],
                lhsT=x_w[g][:, ms].bitcast(FP8X4),
                lhsT_scale=x_sc[:, g, ms],
                rhs=rhs,
                rhs_scale=rhs_sc,
                start=first,
                stop=(which == "c" and g == GROUPS - 1),
            )

        def mx_parts(i, parts, lo=0, hi=WIDE, b=None):
            for g in range(GROUPS):
                for which in parts:
                    mx(i, which, g, lo, hi, b)

        def exp(i, lo=0, hi=WIDE):
            nc.scalar.activation(out=e_t[i // 2][:, i % 2, lo:hi], in_=acc[i, lo][:], func=ACT.Exp)

        def store_y(i):
            j, mt = divmod(i, ROWS)
            nc.sync.dma_start(out=out_0[P * mt : P * (mt + 1), WIDE * j : WIDE * (j + 1)], in_=y_t[i // 2][:, i % 2, :])

        def mul_pair(i):
            j = i // ROWS
            gains = gain_all[:, WIDE * j : WIDE * (j + 1)].unsqueeze(1).to_broadcast([P, 2, WIDE])
            nc.vector.tensor_tensor(out=y_t[i // 2][:], in0=e_t[i // 2][:], in1=gains, op=ALU.mult)
            store_y(i)
            store_y(i + 1)

        def mul(i, lo=0, hi=WIDE):
            j = i // ROWS
            nc.vector.tensor_tensor(
                out=y_t[i // 2][:, i % 2, lo:hi],
                in0=e_t[i // 2][:, i % 2, lo:hi],
                in1=gain_all[:, WIDE * j + lo : WIDE * j + hi],
                op=ALU.mult,
            )
            if hi == WIDE:
                store_y(i)

        def cast_pair(i, copy=nc.vector.tensor_copy):
            copy(
                out=y_bf[i // 2][:].rearrange("m u s (p e) -> m u (s p) e", e=2),
                in_=y_t[i // 2][:].rearrange("m s (p u e) -> m u (s p) e", u=2, e=2),
            )

        def bf_tile(i):
            return last_bf[i % 2] if i >= TILES - 2 else y_bf[i // 2][:, :, i % 2, :]

        def cast(i, lo=0, hi=WIDE):
            nc.vector.tensor_copy(
                out=bf_tile(i)[:, :, lo // 2 : hi // 2].rearrange("m u (p e) -> m u p e", e=2),
                in_=y_t[i // 2][:, i % 2, lo:hi].rearrange("m (p u e) -> m u p e", u=2, e=2),
            )

        turned = {}

        def turn(i, count, b):
            turned[i] = bank(b, [P, count, 2, P])
            for s in range(count):
                for u in range(2):
                    words = bf_tile(i + s)[:, u, :].bitcast(F32)
                    nc.tensor.transpose(turned[i][:, s, u, :], words, ident[:])

        def grp_cols(i, count):
            mt = i % ROWS
            return y_grp[i // ROWS][:, P * PACK * mt : P * PACK * (mt + count)]

        def evac(i, count, copy=nc.scalar.copy):
            copy(
                out=grp_cols(i, count).bitcast(F32).rearrange("p (s m u) -> p s m u", s=count, u=2),
                in_=turned[i][:].rearrange("p s u m -> p s m u"),
            )

        def quant_y(i, count):
            j, mt = divmod(i, ROWS)
            ms = slice(P * mt, P * (mt + count))
            nc.vector.quantize_mx(out=y_w[j][:, ms].bitcast(FP8X4), scales=y_sc[:, j, ms], in_=grp_cols(i, count))

        def store_words(j, lo, hi):
            dst = out_1[j].rearrange("p m t -> p (m t)").bitcast(I32)
            nc.sync.dma_start(out=dst[:, lo:hi], in_=y_w[j][:, lo:hi].bitcast(I32))

        def store_scales(eng, r, lo, hi):
            dst = out_2.rearrange("g (q r) m -> r q g m", r=4)[r]
            eng.dma_start(out=dst[:, lo:hi, :].bitcast(I32), in_=y_sc[r:P:32, lo:hi, :].bitcast(I32))

        load_a(0, 0, 1)
        zero(gain_row[:])
        zero(zeros[:])
        zero(x_sc[:])
        zero(a_sc[0][:])
        zero(b_sc[0][:])
        zero(a_sc[1][:])
        zero(b_sc[1][:])
        zero(ident[:])
        nc.scalar.activation(out=ones[:], in_=zeros[:], func=ACT.Exp)
        nc.sync.dma_start(out=gain_row[0:1, :], in_=gain.rearrange("(o n) -> o n", o=1))
        load_scales(nc.sync, x_sc, 0, x_scales, 0, M)
        load_x(nc.sync, 0)
        load_scales(nc.sync, a_sc[0], 0, a_scales, 0, WIDE)
        load_a(0, 1, 2)
        load_x(nc.sync, 1)
        load_b(0)
        load_scales(nc.sync, b_sc[0], B_ROW, b_scales, 0, WIDE)
        load_c(0, 0)
        make_identity(nc, ident[:], nomemset=True)
        load_c(0, 1)
        load_scales(nc.gpsimd, a_sc[1], 0, a_scales, WIDE, N)
        load_scales(nc.sync, b_sc[1], B_ROW, b_scales, WIDE, N)
        load_c(1, 0)
        load_a(1, 0, 2)
        load_b(1)
        load_c(1, 1)
        load_c(2, 0)
        load_c(2, 1)
        load_a(2, 0, 2)
        load_b(2)

        for j in range(CHUNKS):
            ns = slice(WIDE * j, WIDE * (j + 1))
            spread = bank(5 + j, [P, WIDE])
            nc.tensor.matmul(spread[:], lhsT=ones[:], rhs=gain_row[:, ns], start=True, stop=True)
            nc.scalar.copy(out=gain_all[:, ns], in_=spread[:])

        for j, g in [(0, 0), (0, 1), (1, 0)]:
            weave_s(j, g, 320)
            weave_v(j, g, 320)
            quant_c(j, g)

        for which in "abc":
            for g in range(GROUPS):
                for i in range(ROWS):
                    mx(i, which, g)
        for i in range(4):
            exp(i)
        mul_pair(0)
        weave_s(1, 1)
        weave_v(1, 1)
        cast_pair(0)
        quant_c(1, 1)
        mul_pair(2)
        exp(4)
        exp(5)

        for i in range(6, 9):
            mx_parts(i, "ab")
        weave_s(2, 0)
        mul_pair(4)
        cast_pair(2)
        weave_v(2, 0)
        cast_pair(4)
        quant_c(2, 0)
        for i in range(6, 9):
            mx_parts(i, "c")
            exp(i)
        mul_pair(6)
        weave_s(2, 1, 0)
        mx_parts(9, "abc")
        exp(9)
        quant_c(2, 1)
        cast_pair(6)
        mul_pair(8)
        mx_parts(10, "abc")
        exp(10)
        mx_parts(11, "abc")
        exp(11)
        for s in range(3):
            turn(2 * s, 2, 3 + s)
        for s in range(3):
            evac(2 * s, 2)
        mul_pair(10)
        cast_pair(8)
        quant_y(0, 4)
        quant_y(4, 2)
        store_words(0, 0, M)

        mx_parts(12, "abc")
        exp(12)
        cast_pair(10, nc.scalar.copy)
        mx_parts(13, "abc")
        exp(13)
        mul_pair(12)
        mx_parts(14, "abc")
        exp(14)
        for s in range(3):
            turn(6 + 2 * s, 2, 3 + s)
        mul(14)
        cast_pair(12)
        for s in range(3):
            evac(6 + 2 * s, 2)
        mx_parts(15, "abc")
        exp(15)
        quant_y(6, 4)
        cast(14)
        quant_y(10, 2)
        store_words(1, 0, M)
        for r in range(4):
            store_scales(nc.sync, r, 0, 2)
        mul(15)
        mx_parts(16, "abc")
        exp(16)
        cast(15)
        mul(16)
        for q in range(4):
            mx_parts(17, "abc", P * q, P * (q + 1), q)
            exp(17, P * q, P * (q + 1))
        mul(17, 0, 2 * P)
        cast(16)
        mul(17, 2 * P, WIDE)
        cast(17, 0, 2 * P)
        cast(17, 2 * P, WIDE)
        turn(12, 2, 4)
        turn(14, 2, 5)
        turn(16, 1, 6)
        turn(17, 1, 7)
        evac(12, 2)
        evac(14, 2)
        evac(16, 1, nc.vector.tensor_copy)
        evac(17, 1)
        quant_y(12, 2)
        store_words(2, 0, 2 * P)
        quant_y(14, 2)
        store_words(2, 2 * P, 4 * P)
        quant_y(16, 2)
        store_words(2, 4 * P, M)
        store_scales(nc.scalar, 0, 2, 3)
        store_scales(nc.sync, 1, 2, 3)
        store_scales(nc.scalar, 2, 2, 3)
        store_scales(nc.sync, 3, 2, 3)
